import numpy as np
import ml_dtypes


def mxq(x, axis, fmt="e4m3"):
    dtype, down = {"e4m3": (ml_dtypes.float8_e4m3fn, 7), "e5m2": (ml_dtypes.float8_e5m2, 14)}[fmt]
    v = np.moveaxis(np.asarray(x, np.float32).astype(ml_dtypes.bfloat16).astype(np.float64), axis, -1)
    blocks = v.reshape(v.shape[:-1] + (-1, 32))
    amax = np.abs(blocks).max(-1, keepdims=True)
    byte = np.maximum(np.where(amax > 0, np.frexp(amax)[1] - 1 + 127, 0) - down, 1)
    scale = np.exp2(byte - 127.0)
    codes = (blocks / scale).astype(np.float32).astype(dtype).astype(np.float64)
    return np.moveaxis((codes * scale).reshape(v.shape), -1, axis)


WIDE = False


def mx_kscale(k):
    if not WIDE:
        return np.ones(k)
    levels = np.array([10, -10, 5, -5, 0])
    if k % 512:
        return np.exp2(np.random.permutation(np.resize(levels, k // 32))).repeat(32)
    a = np.empty((k // 512, 16))
    for p in range(k // 512):
        a[p, :8] = np.random.permutation(np.resize(levels, 8))
        for g in range(8):
            far = levels[np.abs(levels - a[p, g]) >= 10]
            a[p, g + 8] = far[np.random.randint(len(far))]
    return np.exp2(a.ravel()).repeat(32)


def f64(x):
    return np.asarray(x).astype(np.float64)


def striped(idx):
    return np.tile(idx.reshape(-1, 16).T, (8, 1)).astype(np.uint16)


def unstriped(offs):
    return offs[:16].T.reshape(-1).astype(np.int64)


def pack_weight(w):
    k, n = w.shape
    w = f64(np.asarray(w, np.float32).astype(ml_dtypes.bfloat16)).reshape(k // 32, 32, n)
    amax = np.abs(w).max(1)
    byte = np.clip(np.where(amax > 0, np.frexp(amax)[1] - 1 + 127 - 7, 1), 1, 254)
    scaled = (w * np.exp2(127.0 - byte)[:, None, :]).reshape(k, n).astype(np.float32)
    words = np.ascontiguousarray(scaled.reshape(k // 512, 128, 4, n).transpose(0, 1, 3, 2)).astype(ml_dtypes.float8_e4m3fn).view(np.uint8)
    return words, np.ascontiguousarray(byte.astype(np.uint8).reshape(k // 512, 16, n))


def unpack_weight(words, scales):
    g, p, n, _ = words.shape
    vals = np.ascontiguousarray(words).view(ml_dtypes.float8_e4m3fn).astype(np.float64) * np.repeat(np.exp2(scales.astype(np.float64) - 127.0), 8, axis=1)[..., None]
    return vals.transpose(0, 1, 3, 2).reshape(g * 512, n)


K, T, S, D, N, V, R = 1024, 4096, 1024, 4, 128, 256, 128
P = 2 ** 7


def setup_inputs():
    n = np.random.standard_normal
    s = mx_kscale(K)[:, None]
    packed_xT = pack_weight(n((K, T)) * s)
    return {
        "x_words": packed_xT[0],
        "x_scales": packed_xT[1],
        "w1": (n((K, N)) / np.sqrt(K) / s).astype(np.float32),
        "w2": (n((K, N)) / np.sqrt(K) / s).astype(np.float32),
        "rad": (np.random.uniform(0.3, 1.2, (N, 1))).astype(np.float32),
        "fov": (np.tile(np.random.uniform(0.3, 1.0, S), (P, 1))).astype(np.float32),
        "want": (n((N, V))).astype(np.float32),
        "vel": (n((N, V))).astype(np.float32),
        "relax": (np.random.uniform(0.1, 0.6, (N, 1))).astype(np.float32),
        "offs": striped(np.random.permutation(T)[:S]),
        "lead": striped(np.random.permutation(V)[:R]),
        "who": striped(np.random.permutation(V)[:R]),
    }


def reference(x_words, x_scales, w1, w2, rad, fov, want, vel, relax, offs, lead, who):
    xq = unpack_weight(x_words, x_scales)[:, unstriped(offs)]
    y = mxq(f64(w1), 0, "e4m3").T @ xq
    z = mxq(f64(w2), 0, "e4m3").T @ xq
    ds = np.sqrt((y) ** 2 + (z) ** 2 + 0.1)
    st = (np.exp(-1.0 * ds + f64(rad))) * f64(fov)[:1]
    fx = (st * y) / ds
    ff = fx.reshape(len(fx), -1, D).sum(axis=2)
    nv = f64(vel) + f64(relax) * (f64(want) - f64(vel)) + 1.5 * ff
    return 0.7 * nv[:, unstriped(who)] + 0.3 * nv[:, unstriped(lead)]

@@ -1,0 +1,190 @@
+from contextlib import ExitStack
+
+import concourse.mybir as mybir
+
+F32 = mybir.dt.float32
+BF16 = mybir.dt.bfloat16
+I32 = mybir.dt.int32
+U32 = mybir.dt.uint32
+U16 = mybir.dt.uint16
+U8 = mybir.dt.uint8
+FP8X4 = mybir.dt.float8_e4m3fn_x4
+ALU = mybir.AluOpType
+ACT = mybir.ActivationFunctionType
+
+P = 128
+K, T, S, D, M, V, R = 1024, 4096, 1024, 4, 128, 256, 128
+PACK = 4
+K_PASS = P * PACK
+PASSES = K // K_PASS
+HALF = 512
+HALVES = S // HALF
+GROUP = 16
+
+FLOPS = 2 * 2 * K * M * S
+
+
+def tile_picked_ysocf_lead_p_kernel(
+    tc, x_words, x_scales, w1, w2, rad, fov, want, vel, relax, offs, lead, who, out
+):
+    nc = tc.nc
+    with ExitStack() as ctx:
+        keep = ctx.enter_context(tc.tile_pool(name="keep", bufs=1))
+        psum = ctx.enter_context(tc.psum_pool(name="psum", bufs=1))
+
+        def sb(name, shape, dtype):
+            return keep.tile(shape, dtype, name=name, align_bytes=64)
+
+        offs_sb = sb("offs_sb", [P, S // GROUP], U16)
+        who_sb = sb("who_sb", [P, R // GROUP], U16)
+        lead_sb = sb("lead_sb", [P, R // GROUP], U16)
+        words = [sb("words%d" % o, [P, T], U32) for o in range(PASSES)]
+        planes = sb("planes", [P, T], U8)
+        w_raw = [[sb("w_raw%d%d" % (i, o), [P, PACK, M], F32) for o in range(PASSES)] for i in range(2)]
+        fov_sb = sb("fov_sb", [P, S], F32)
+        vel_sb = sb("vel_sb", [P, V], F32)
+        want_sb = sb("want_sb", [P, V], F32)
+        rad_sb = sb("rad_sb", [P, 1], F32)
+        relax_sb = sb("relax_sb", [P, 1], F32)
+
+        ones = sb("ones", [P, R], F32)
+        ratio = sb("ratio", [P, R], F32)
+        warm = sb("warm", [P, 1], F32)
+        nc.gpsimd.memset(planes[:].bitcast(I32), 0)
+        nc.vector.memset(ones[:], 1.0)
+        nc.scalar.activation(warm[:], ones[:, 0:1], ACT.Abs_reciprocal_sqrt)
+        nc.vector.tensor_scalar(ratio[:], ones[:], 0.7 / 0.3, None, ALU.mult)
+
+        def load_words(o):
+            nc.sync.dma_start(words[o][:].bitcast(I32), x_words[o].rearrange("p n t -> p (n t)").bitcast(I32))
+
+        def load_w(i, o):
+            rows = (w1, w2)[i][o * K_PASS : (o + 1) * K_PASS, :]
+            nc.sync.dma_start(w_raw[i][o][:], rows.rearrange("(p j) n -> p j n", j=PACK))
+
+        nc.sync.dma_start(offs_sb[:], offs)
+        load_words(0)
+        for q in range(4):
+            nc.gpsimd.dma_start(
+                planes[32 * q : 32 * q + 4 * PASSES, :].bitcast(I32),
+                x_scales[:, 4 * q : 4 * q + 4, :].bitcast(I32),
+            )
+        load_w(0, 0)
+        load_w(1, 0)
+        load_w(0, 1)
+        load_words(1)
+        load_w(1, 1)
+        nc.sync.dma_start(relax_sb[:], relax)
+        nc.sync.dma_start(vel_sb[:], vel)
+        nc.sync.dma_start(fov_sb[:], fov)
+        nc.sync.dma_start(want_sb[:], want)
+        nc.sync.dma_start(rad_sb[:], rad)
+        nc.sync.dma_start(who_sb[:], who)
+        nc.sync.dma_start(lead_sb[:], lead)
+
+        w_codes = [[sb("w_codes%d%d" % (i, o), [P, M], U32) for o in range(PASSES)] for i in range(2)]
+        w_planes = [[sb("w_planes%d%d" % (i, o), [P, M], U8) for o in range(PASSES)] for i in range(2)]
+        w_bf = [[sb("w_bf%d%d" % (i, o), [P, M, PACK], BF16) for o in range(PASSES)] for i in range(2)]
+
+        def round_w(i, o):
+            nc.scalar.copy(
+                w_bf[i][o][:].rearrange("p (c e) j -> p c j e", e=4),
+                w_raw[i][o][:].rearrange("p j (c e) -> p c j e", e=4),
+            )
+
+        def quantize_w(i, o):
+            nc.vector.quantize_mx(
+                w_codes[i][o][:].bitcast(FP8X4), w_planes[i][o][:], w_bf[i][o][:].rearrange("p n j -> p (n j)")
+            )
+
+        picked = [[sb("picked%d%d" % (o, h), [P, HALF], U32) for h in range(HALVES)] for o in range(PASSES)]
+        picked_planes = [sb("picked_planes%d" % h, [P, HALF], U8) for h in range(HALVES)]
+        acc = [[psum.tile([M, HALF], F32, name="acc%d%d" % (i, h)) for h in range(HALVES)] for i in range(2)]
+
+        def entries(h):
+            return offs_sb[:, h * HALF // GROUP : (h + 1) * HALF // GROUP]
+
+        def pick_words(o, h):
+            nc.vector.tensor_copy(picked[o][h][:], words[o][:].indirect(entries(h)))
+
+        def pick_planes(h):
+            nc.vector.tensor_copy(picked_planes[h][:], planes[:].indirect(entries(h)))
+
+        def product(i, o, h):
+            nc.tensor.matmul_mx(
+                acc[i][h][:],
+                lhsT=w_codes[i][o][:].bitcast(FP8X4),
+                lhsT_scale=w_planes[i][o][:],
+                rhs=picked[o][h][:].bitcast(FP8X4),
+                rhs_scale=picked_planes[h][4 * o : P, :],
+                start=(o == 0),
+                stop=(o == PASSES - 1),
+            )
+
+        for i, o in ((0, 0), (1, 0), (0, 1), (1, 1)):
+            round_w(i, o)
+        for h in range(HALVES):
+            pick_words(0, h)
+        for i, o in ((0, 0), (1, 0), (0, 1)):
+            quantize_w(i, o)
+        for h in range(HALVES):
+            pick_planes(h)
+            product(0, 0, h)
+            product(1, 0, h)
+        pick_words(1, 0)
+        product(0, 1, 0)
+        quantize_w(1, 1)
+        product(1, 1, 0)
+        pick_words(1, 1)
+        product(0, 1, 1)
+        product(1, 1, 1)
+
+        def halves(name):
+            return [sb("%s%d" % (name, h), [P, HALF], F32) for h in range(HALVES)]
+
+        y_sq, z_sq, ssq, inv, dist, y_fov, pull, force = (
+            halves(n) for n in ("y_sq", "z_sq", "ssq", "inv", "dist", "y_fov", "pull", "force")
+        )
+        decay = [ssq[1], ssq[0]]
+
+        for h in range(HALVES):
+            nc.scalar.activation(y_sq[h][:], acc[0][h][:], ACT.Square)
+            nc.scalar.activation(z_sq[h][:], acc[1][h][:], ACT.Square)
+            nc.vector.scalar_tensor_tensor(ssq[h][:], y_sq[h][:], 0.1, z_sq[h][:], ALU.add, ALU.add)
+            nc.vector.scalar_tensor_tensor(
+                y_fov[h][:], acc[0][h][:], 0.3 * 1.5, fov_sb[:, h * HALF : (h + 1) * HALF], ALU.mult, ALU.mult
+            )
+        for h in range(HALVES):
+            nc.scalar.activation(inv[h][:], ssq[h][:], ACT.Abs_reciprocal_sqrt)
+            nc.vector.tensor_tensor(dist[h][:], ssq[h][:], inv[h][:], ALU.mult)
+        for h in range(HALVES):
+            nc.vector.tensor_tensor(pull[h][:], y_fov[h][:], inv[h][:], ALU.mult)
+
+        c_want = sb("c_want", [P, 1], F32)
+        c_vel = sb("c_vel", [P, 1], F32)
+        vel_part = sb("vel_part", [P, V], F32)
+        base = sb("base", [P, V], F32)
+        summed = sb("summed", [P, V], F32)
+        new_vel = sb("new_vel", [P, V], F32)
+        own = sb("own", [P, R], F32)
+        result = sb("result", [P, R], F32)
+        nc.gpsimd.tensor_scalar(c_want[:], relax_sb[:], 0.3, 0.0, ALU.mult, ALU.add)
+        nc.gpsimd.tensor_scalar(c_vel[:], relax_sb[:], -0.3, 0.3, ALU.mult, ALU.add)
+        nc.scalar.activation(vel_part[:], vel_sb[:], ACT.Copy, scale=c_vel[:])
+        nc.vector.scalar_tensor_tensor(base[:], want_sb[:], c_want[:], vel_part[:], ALU.mult, ALU.add)
+
+        for h in range(HALVES):
+            nc.scalar.activation(decay[h][:], dist[h][:], ACT.Exp, bias=rad_sb[:], scale=-1.0)
+        for h in range(HALVES):
+            nc.vector.tensor_tensor(force[h][:], pull[h][:], decay[h][:], ALU.mult)
+        for h in range(HALVES):
+            nc.vector.tensor_reduce(
+                summed[:, h * HALF // D : (h + 1) * HALF // D],
+                force[h][:].rearrange("p (v d) -> p v d", d=D),
+                mybir.AxisListType.X,
+                ALU.add,
+            )
+        nc.vector.tensor_tensor(new_vel[:], summed[:], base[:], ALU.add)
+        nc.vector.tensor_tensor(own[:], new_vel[:].indirect(who_sb[:]), ratio[:], ALU.mult)
+        nc.vector.tensor_tensor(result[:], new_vel[:].indirect(lead_sb[:]), own[:], ALU.add)
+        nc.sync.dma_start(out, result[:])

@@ -1,6 +1,7 @@
 from contextlib import ExitStack
 
 import concourse.mybir as mybir
+from concourse.masks import make_identity
 
 F32 = mybir.dt.float32
 BF16 = mybir.dt.bfloat16
@@ -20,6 +21,9 @@ PASSES = K // K_PASS
 HALF = 512
 HALVES = S // HALF
 GROUP = 16
+QUARTER = 256
+QUARTERS = S // QUARTER
+BANK = 512
 
 FLOPS = 2 * 2 * K * M * S
 
@@ -32,16 +36,19 @@ def tile_picked_ysocf_lead_p_kernel(
         keep = ctx.enter_context(tc.tile_pool(name="keep", bufs=1))
         psum = ctx.enter_context(tc.psum_pool(name="psum", bufs=1))
 
-        def sb(name, shape, dtype):
-            return keep.tile(shape, dtype, name=name, align_bytes=64)
+        def sb(name, shape, dtype, tag=None):
+            return keep.tile(shape, dtype, name=name, tag=tag or name, align_bytes=64)
 
         offs_sb = sb("offs_sb", [P, S // GROUP], U16)
         who_sb = sb("who_sb", [P, R // GROUP], U16)
         lead_sb = sb("lead_sb", [P, R // GROUP], U16)
         words = [sb("words%d" % o, [P, T], U32) for o in range(PASSES)]
         planes = sb("planes", [P, T], U8)
-        w_raw = [[sb("w_raw%d%d" % (i, o), [P, PACK, M], F32) for o in range(PASSES)] for i in range(2)]
-        fov_sb = sb("fov_sb", [P, S], F32)
+        w1_raw = sb("w1_raw", [P, PASSES, PACK, M], F32)
+        w2_raw = [sb("w2_raw%d" % o, [P, 1, PACK, M], F32) for o in range(PASSES)]
+        fov_cols = sb("fov_cols", [P, HALVES, D], F32)
+        fov_rows = [sb("fov_rows%d" % h, [P, D, P], F32) for h in range(HALVES)]
+        ident = sb("ident", [P, P], F32)
         vel_sb = sb("vel_sb", [P, V], F32)
         want_sb = sb("want_sb", [P, V], F32)
         rad_sb = sb("rad_sb", [P, 1], F32)
@@ -50,7 +57,8 @@ def tile_picked_ysocf_lead_p_kernel(
         ones = sb("ones", [P, R], F32)
         ratio = sb("ratio", [P, R], F32)
         warm = sb("warm", [P, 1], F32)
-        nc.gpsimd.memset(planes[:].bitcast(I32), 0)
+        nc.gpsimd.memset(planes[:, 0 : T // 2].bitcast(I32), 0)
+        nc.vector.memset(planes[:, T // 2 : T].bitcast(I32), 0)
         nc.vector.memset(ones[:], 1.0)
         nc.scalar.activation(warm[:], ones[:, 0:1], ACT.Abs_reciprocal_sqrt)
         nc.vector.tensor_scalar(ratio[:], ones[:], 0.7 / 0.3, None, ALU.mult)
@@ -58,133 +66,168 @@ def tile_picked_ysocf_lead_p_kernel(
         def load_words(o):
             nc.sync.dma_start(words[o][:].bitcast(I32), x_words[o].rearrange("p n t -> p (n t)").bitcast(I32))
 
-        def load_w(i, o):
-            rows = (w1, w2)[i][o * K_PASS : (o + 1) * K_PASS, :]
-            nc.sync.dma_start(w_raw[i][o][:], rows.rearrange("(p j) n -> p j n", j=PACK))
+        def load_w(raw, rows):
+            nc.sync.dma_start(
+                raw[:].rearrange("p o j n -> p o (j n)"), rows.rearrange("(o p j) n -> p o (j n)", p=P, j=PACK)
+            )
 
         nc.sync.dma_start(offs_sb[:], offs)
+        nc.sync.dma_start(relax_sb[:], relax)
         load_words(0)
+        nc.sync.dma_start(fov_cols[:], fov[0, :].rearrange("(h v d) -> v h d", h=HALVES, d=D))
+        load_w(w1_raw, w1)
         for q in range(4):
-            nc.gpsimd.dma_start(
+            nc.sync.dma_start(
                 planes[32 * q : 32 * q + 4 * PASSES, :].bitcast(I32),
                 x_scales[:, 4 * q : 4 * q + 4, :].bitcast(I32),
             )
-        load_w(0, 0)
-        load_w(1, 0)
-        load_w(0, 1)
+        load_w(w2_raw[0], w2[0:K_PASS, :])
         load_words(1)
-        load_w(1, 1)
-        nc.sync.dma_start(relax_sb[:], relax)
+        load_w(w2_raw[1], w2[K_PASS:K, :])
         nc.sync.dma_start(vel_sb[:], vel)
-        nc.sync.dma_start(fov_sb[:], fov)
         nc.sync.dma_start(want_sb[:], want)
         nc.sync.dma_start(rad_sb[:], rad)
         nc.sync.dma_start(who_sb[:], who)
         nc.sync.dma_start(lead_sb[:], lead)
 
-        w_codes = [[sb("w_codes%d%d" % (i, o), [P, M], U32) for o in range(PASSES)] for i in range(2)]
-        w_planes = [[sb("w_planes%d%d" % (i, o), [P, M], U8) for o in range(PASSES)] for i in range(2)]
-        w_bf = [[sb("w_bf%d%d" % (i, o), [P, M, PACK], BF16) for o in range(PASSES)] for i in range(2)]
-
-        def round_w(i, o):
+        def round_w(name, raw):
+            rounded = sb(name, [P, raw.shape[1], M, PACK], BF16)
             nc.scalar.copy(
-                w_bf[i][o][:].rearrange("p (c e) j -> p c j e", e=4),
-                w_raw[i][o][:].rearrange("p j (c e) -> p c j e", e=4),
+                rounded[:].rearrange("p o (c e) j -> p o c j e", e=4),
+                raw[:].rearrange("p o j (c e) -> p o c j e", e=4),
             )
+            return rounded
 
-        def quantize_w(i, o):
-            nc.vector.quantize_mx(
-                w_codes[i][o][:].bitcast(FP8X4), w_planes[i][o][:], w_bf[i][o][:].rearrange("p n j -> p (n j)")
-            )
+        def quantize_w(name, rounded):
+            passes = rounded.shape[1]
+            codes = sb(name + "_codes", [P, passes * M], U32)
+            scales = sb(name + "_scales", [P, passes * M], U8)
+            nc.vector.quantize_mx(codes[:].bitcast(FP8X4), scales[:], rounded[:].rearrange("p o n j -> p (o n j)"))
+            return [(codes[:, o * M : (o + 1) * M], scales[:, o * M : (o + 1) * M]) for o in range(passes)]
 
-        picked = [[sb("picked%d%d" % (o, h), [P, HALF], U32) for h in range(HALVES)] for o in range(PASSES)]
+        picked = {}
         picked_planes = [sb("picked_planes%d" % h, [P, HALF], U8) for h in range(HALVES)]
-        acc = [[psum.tile([M, HALF], F32, name="acc%d%d" % (i, h)) for h in range(HALVES)] for i in range(2)]
+        banks = [[psum.tile([M, BANK], F32, name="bank%d%d" % (i, q)) for q in range(QUARTERS)] for i in range(2)]
+        acc = [[banks[i][q][:, 0:QUARTER] for q in range(QUARTERS)] for i in range(2)]
+
+        make_identity(nc, ident[:])
+        for h in range(HALVES):
+            spread = banks[1][QUARTERS - HALVES + h]
+            for d in range(D):
+                nc.tensor.transpose(
+                    spread[:, d * P : (d + 1) * P], fov_cols[:, h, d : d + 1].to_broadcast([P, P]), ident[:]
+                )
+            nc.scalar.activation(
+                fov_rows[h][:].rearrange("p d v -> p (d v)"), spread[:], ACT.Copy, scale=0.3 * 1.5
+            )
 
         def entries(h):
             return offs_sb[:, h * HALF // GROUP : (h + 1) * HALF // GROUP]
 
-        def pick_words(o, h):
-            nc.vector.tensor_copy(picked[o][h][:], words[o][:].indirect(entries(h)))
+        def pick_words(o, h, tag=None):
+            picked[o, h] = sb("picked%d%d" % (o, h), [P, HALF], U32, tag)
+            nc.vector.tensor_copy(picked[o, h][:], words[o][:].indirect(entries(h)))
 
         def pick_planes(h):
             nc.vector.tensor_copy(picked_planes[h][:], planes[:].indirect(entries(h)))
 
-        def product(i, o, h):
+        def product(i, o, q, weights):
+            h, cols = q // 2, slice(q % 2 * QUARTER, (q % 2 + 1) * QUARTER)
             nc.tensor.matmul_mx(
-                acc[i][h][:],
-                lhsT=w_codes[i][o][:].bitcast(FP8X4),
-                lhsT_scale=w_planes[i][o][:],
-                rhs=picked[o][h][:].bitcast(FP8X4),
-                rhs_scale=picked_planes[h][4 * o : P, :],
+                acc[i][q],
+                lhsT=weights[o][0].bitcast(FP8X4),
+                lhsT_scale=weights[o][1],
+                rhs=picked[o, h][:, cols].bitcast(FP8X4),
+                rhs_scale=picked_planes[h][4 * o : P, cols],
                 start=(o == 0),
                 stop=(o == PASSES - 1),
             )
 
-        for i, o in ((0, 0), (1, 0), (0, 1), (1, 1)):
-            round_w(i, o)
+        w1_rounded = round_w("w1_rounded", w1_raw)
+        w2_rounded = [round_w("w2_rounded%d" % o, w2_raw[o]) for o in range(PASSES)]
         for h in range(HALVES):
             pick_words(0, h)
-        for i, o in ((0, 0), (1, 0), (0, 1)):
-            quantize_w(i, o)
+        w1_mx = quantize_w("w1", w1_rounded)
+        w2_mx = quantize_w("w20", w2_rounded[0])
         for h in range(HALVES):
             pick_planes(h)
-            product(0, 0, h)
-            product(1, 0, h)
-        pick_words(1, 0)
-        product(0, 1, 0)
-        quantize_w(1, 1)
-        product(1, 1, 0)
-        pick_words(1, 1)
-        product(0, 1, 1)
-        product(1, 1, 1)
-
-        def halves(name):
-            return [sb("%s%d" % (name, h), [P, HALF], F32) for h in range(HALVES)]
-
-        y_sq, z_sq, ssq, inv, dist, y_fov, pull, force = (
-            halves(n) for n in ("y_sq", "z_sq", "ssq", "inv", "dist", "y_fov", "pull", "force")
-        )
-        decay = [ssq[1], ssq[0]]
-
+            for q in (2 * h, 2 * h + 1):
+                product(0, 0, q, w1_mx)
+                product(1, 0, q, w2_mx)
         for h in range(HALVES):
-            nc.scalar.activation(y_sq[h][:], acc[0][h][:], ACT.Square)
-            nc.scalar.activation(z_sq[h][:], acc[1][h][:], ACT.Square)
-            nc.vector.scalar_tensor_tensor(ssq[h][:], y_sq[h][:], 0.1, z_sq[h][:], ALU.add, ALU.add)
-            nc.vector.scalar_tensor_tensor(
-                y_fov[h][:], acc[0][h][:], 0.3 * 1.5, fov_sb[:, h * HALF : (h + 1) * HALF], ALU.mult, ALU.mult
-            )
-        for h in range(HALVES):
-            nc.scalar.activation(inv[h][:], ssq[h][:], ACT.Abs_reciprocal_sqrt)
-            nc.vector.tensor_tensor(dist[h][:], ssq[h][:], inv[h][:], ALU.mult)
-        for h in range(HALVES):
-            nc.vector.tensor_tensor(pull[h][:], y_fov[h][:], inv[h][:], ALU.mult)
+            pick_words(1, h)
+            for q in (2 * h, 2 * h + 1):
+                product(0, 1, q, w1_mx)
+        w2_mx = w2_mx + quantize_w("w21", w2_rounded[1])
+        for q in range(QUARTERS):
+            product(1, 1, q, w2_mx)
+
+        VQ = QUARTER // D
+        VH = HALF // D
+
+        def pieces(name, count, width):
+            return [sb("%s%d" % (name, n), [P, D, width], F32) for n in range(count)]
+
+        z_sq = pieces("z_sq", QUARTERS, VQ)
+        ssq, inv = (pieces(n, HALVES, VH) for n in ("ssq", "inv"))
+        dist = sb("dist", [P, D, V], F32)
+        pull = sb("pull", [P, D, V], F32)
+        decay = [sb("decay%d" % d, [P, V], F32) for d in range(D)]
+        force = [sb("force%d" % d, [P, V], F32) for d in range(D)]
+        partial = [sb("partial%d" % d, [P, V], F32) for d in range(D)]
 
         c_want = sb("c_want", [P, 1], F32)
         c_vel = sb("c_vel", [P, 1], F32)
         vel_part = sb("vel_part", [P, V], F32)
-        base = sb("base", [P, V], F32)
-        summed = sb("summed", [P, V], F32)
-        new_vel = sb("new_vel", [P, V], F32)
+        base = sb("base", [P, V], F32, "w2_rounded1")
         own = sb("own", [P, R], F32)
         result = sb("result", [P, R], F32)
         nc.gpsimd.tensor_scalar(c_want[:], relax_sb[:], 0.3, 0.0, ALU.mult, ALU.add)
         nc.gpsimd.tensor_scalar(c_vel[:], relax_sb[:], -0.3, 0.3, ALU.mult, ALU.add)
         nc.scalar.activation(vel_part[:], vel_sb[:], ACT.Copy, scale=c_vel[:])
-        nc.vector.scalar_tensor_tensor(base[:], want_sb[:], c_want[:], vel_part[:], ALU.mult, ALU.add)
+        want_part = sb("want_part", [P, V], F32)
+        nc.scalar.activation(want_part[:], want_sb[:], ACT.Copy, scale=c_want[:])
+        nc.gpsimd.tensor_tensor(base[:], want_part[:], vel_part[:], ALU.add)
 
+        y_sq = [sb("y_sq%d" % h, [P, 2, D, VQ], F32, ("vel_sb", "want_sb")[h]) for h in range(HALVES)]
+
+        def by_neighbour(bank):
+            return bank.rearrange("p (v d) -> p d v", d=D)
+
+        for q in range(QUARTERS):
+            nc.scalar.activation(y_sq[q // 2][:, q % 2], by_neighbour(acc[0][q]), ACT.Square)
+        for q in range(QUARTERS):
+            h, cols = q // 2, slice(q % 2 * VQ, (q % 2 + 1) * VQ)
+            nc.scalar.activation(z_sq[q][:], by_neighbour(acc[1][q]), ACT.Square)
+            nc.vector.scalar_tensor_tensor(ssq[h][:, :, cols], y_sq[h][:, q % 2], 0.1, z_sq[q][:], ALU.add, ALU.add)
+        y_fov_head = sb("y_fov_head", [P, D, V - VQ], F32)
+        y_fov_last = sb("y_fov_last", [P, D, VQ], F32, "z_sq%d" % (QUARTERS - 1))
+        for q in range(QUARTERS):
+            h, cols = q // 2, slice(q % 2 * VQ, (q % 2 + 1) * VQ)
+            dst = y_fov_last[:] if q == QUARTERS - 1 else y_fov_head[:, :, q * VQ : (q + 1) * VQ]
+            nc.vector.tensor_tensor(dst, by_neighbour(acc[0][q]), fov_rows[h][:, :, cols], ALU.mult)
         for h in range(HALVES):
-            nc.scalar.activation(decay[h][:], dist[h][:], ACT.Exp, bias=rad_sb[:], scale=-1.0)
-        for h in range(HALVES):
-            nc.vector.tensor_tensor(force[h][:], pull[h][:], decay[h][:], ALU.mult)
-        for h in range(HALVES):
-            nc.vector.tensor_reduce(
-                summed[:, h * HALF // D : (h + 1) * HALF // D],
-                force[h][:].rearrange("p (v d) -> p v d", d=D),
-                mybir.AxisListType.X,
-                ALU.add,
-            )
-        nc.vector.tensor_tensor(new_vel[:], summed[:], base[:], ALU.add)
+            nc.scalar.activation(inv[h][:], ssq[h][:], ACT.Abs_reciprocal_sqrt)
+            nc.vector.tensor_tensor(dist[:, :, h * VH : (h + 1) * VH], ssq[h][:], inv[h][:], ALU.mult)
+        nc.vector.tensor_tensor(pull[:, :, 0:VH], y_fov_head[:, :, 0:VH], inv[0][:], ALU.mult)
+        nc.vector.tensor_tensor(pull[:, :, VH : V - VQ], y_fov_head[:, :, VH : V - VQ], inv[1][:, :, 0:VQ], ALU.mult)
+        nc.vector.tensor_tensor(pull[:, :, V - VQ : V], y_fov_last[:], inv[1][:, :, VQ:VH], ALU.mult)
+
+        for d in range(D):
+            nc.scalar.activation(decay[d][:], dist[:, d, :], ACT.Exp, bias=rad_sb[:], scale=-1.0)
+
+        def multiply(d):
+            nc.vector.tensor_tensor(force[d][:], pull[:, d, :], decay[d][:], ALU.mult)
+
+        def add_up(d):
+            nc.vector.tensor_tensor(partial[d][:], force[d][:], partial[d - 1][:] if d else base[:], ALU.add)
+
+        multiply(0)
+        for d in range(1, D):
+            multiply(d)
+            add_up(d - 1)
+        add_up(D - 1)
+        new_vel = partial[D - 1]
         nc.vector.tensor_tensor(own[:], new_vel[:].indirect(who_sb[:]), ratio[:], ALU.mult)
         nc.vector.tensor_tensor(result[:], new_vel[:].indirect(lead_sb[:]), own[:], ALU.add)
         nc.sync.dma_start(out, result[:])

@@ -46,8 +46,8 @@ def tile_picked_ysocf_lead_p_kernel(
         planes = sb("planes", [P, T], U8)
         w1_raw = sb("w1_raw", [P, PASSES, PACK, M], F32)
         w2_raw = [sb("w2_raw%d" % o, [P, 1, PACK, M], F32) for o in range(PASSES)]
-        fov_cols = sb("fov_cols", [P, HALVES, D], F32)
-        fov_rows = [sb("fov_rows%d" % h, [P, D, P], F32) for h in range(HALVES)]
+        fov_cols = sb("fov_cols", [P, 2 * D], F32)
+        fov_rows = sb("fov_rows", [P, D, V], F32)
         ident = sb("ident", [P, P], F32)
         vel_sb = sb("vel_sb", [P, V], F32)
         want_sb = sb("want_sb", [P, V], F32)
@@ -71,10 +71,9 @@ def tile_picked_ysocf_lead_p_kernel(
                 raw[:].rearrange("p o j n -> p o (j n)"), rows.rearrange("(o p j) n -> p o (j n)", p=P, j=PACK)
             )
 
-        nc.sync.dma_start(offs_sb[:], offs)
-        nc.sync.dma_start(relax_sb[:], relax)
         load_words(0)
-        nc.sync.dma_start(fov_cols[:], fov[0, :].rearrange("(h v d) -> v h d", h=HALVES, d=D))
+        nc.sync.dma_start(offs_sb[:], offs)
+        nc.sync.dma_start(fov_cols[:], fov[0, :].rearrange("(p e) -> p e", p=P))
         load_w(w1_raw, w1)
         for q in range(4):
             nc.sync.dma_start(
@@ -83,6 +82,7 @@ def tile_picked_ysocf_lead_p_kernel(
             )
         load_w(w2_raw[0], w2[0:K_PASS, :])
         load_words(1)
+        nc.sync.dma_start(relax_sb[:], relax)
         load_w(w2_raw[1], w2[K_PASS:K, :])
         nc.sync.dma_start(vel_sb[:], vel)
         nc.sync.dma_start(want_sb[:], want)
@@ -111,14 +111,16 @@ def tile_picked_ysocf_lead_p_kernel(
         acc = [[banks[i][q][:, 0:QUARTER] for q in range(QUARTERS)] for i in range(2)]
 
         make_identity(nc, ident[:])
-        for h in range(HALVES):
-            spread = banks[1][QUARTERS - HALVES + h]
-            for d in range(D):
-                nc.tensor.transpose(
-                    spread[:, d * P : (d + 1) * P], fov_cols[:, h, d : d + 1].to_broadcast([P, P]), ident[:]
-                )
+        for b in range(2):
+            spread = banks[1][QUARTERS - 2 + b]
+            for n, (u, d) in enumerate((u, d) for u in range(2) for d in (2 * b, 2 * b + 1)):
+                column = fov_cols[:, D * u + d : D * u + d + 1]
+                nc.tensor.transpose(spread[:, n * P : (n + 1) * P], column.to_broadcast([P, P]), ident[:])
             nc.scalar.activation(
-                fov_rows[h][:].rearrange("p d v -> p (d v)"), spread[:], ACT.Copy, scale=0.3 * 1.5
+                fov_rows[:, 2 * b : 2 * b + 2, :].rearrange("p d (w u) -> p d w u", u=2),
+                spread[:].rearrange("p (u d w) -> p d w u", u=2, d=2),
+                ACT.Copy,
+                scale=0.3 * 1.5,
             )
 
         def entries(h):
@@ -203,9 +205,8 @@ def tile_picked_ysocf_lead_p_kernel(
         y_fov_head = sb("y_fov_head", [P, D, V - VQ], F32)
         y_fov_last = sb("y_fov_last", [P, D, VQ], F32, "z_sq%d" % (QUARTERS - 1))
         for q in range(QUARTERS):
-            h, cols = q // 2, slice(q % 2 * VQ, (q % 2 + 1) * VQ)
             dst = y_fov_last[:] if q == QUARTERS - 1 else y_fov_head[:, :, q * VQ : (q + 1) * VQ]
-            nc.vector.tensor_tensor(dst, by_neighbour(acc[0][q]), fov_rows[h][:, :, cols], ALU.mult)
+            nc.vector.tensor_tensor(dst, by_neighbour(acc[0][q]), fov_rows[:, :, q * VQ : (q + 1) * VQ], ALU.mult)
         for h in range(HALVES):
             nc.scalar.activation(inv[h][:], ssq[h][:], ACT.Abs_reciprocal_sqrt)
             nc.vector.tensor_tensor(dist[:, :, h * VH : (h + 1) * VH], ssq[h][:], inv[h][:], ALU.mult)
@@ -228,6 +229,10 @@ def tile_picked_ysocf_lead_p_kernel(
             add_up(d - 1)
         add_up(D - 1)
         new_vel = partial[D - 1]
-        nc.vector.tensor_tensor(own[:], new_vel[:].indirect(who_sb[:]), ratio[:], ALU.mult)
-        nc.vector.tensor_tensor(result[:], new_vel[:].indirect(lead_sb[:]), own[:], ALU.add)
+        walkers = [slice(n * R // 2, (n + 1) * R // 2) for n in range(2)]
+        columns = [slice(n * R // 2 // GROUP, (n + 1) * R // 2 // GROUP) for n in range(2)]
+        for cols, picks in zip(walkers, columns):
+            nc.vector.tensor_tensor(own[:, cols], new_vel[:].indirect(who_sb[:, picks]), ratio[:, cols], ALU.mult)
+        for cols, picks in zip(walkers, columns):
+            nc.vector.tensor_tensor(result[:, cols], new_vel[:].indirect(lead_sb[:, picks]), own[:, cols], ALU.add)
         nc.sync.dma_start(out, result[:])

@@ -18,12 +18,18 @@ K, T, S, D, M, V, R = 1024, 4096, 1024, 4, 128, 256, 128
 PACK = 4
 K_PASS = P * PACK
 PASSES = K // K_PASS
+GROUP = 16
 HALF = 512
 HALVES = S // HALF
-GROUP = 16
 QUARTER = 256
 QUARTERS = S // QUARTER
 BANK = 512
+QUADRANT = 32
+ROWS = 4
+VQ = QUARTER // D
+VH = HALF // D
+V_HEAD = V - VQ
+KEPT = 0.3
 
 FLOPS = 2 * 2 * K * M * S
 
@@ -42,59 +48,63 @@ def tile_picked_ysocf_lead_p_kernel(
         offs_sb = sb("offs_sb", [P, S // GROUP], U16)
         who_sb = sb("who_sb", [P, R // GROUP], U16)
         lead_sb = sb("lead_sb", [P, R // GROUP], U16)
-        words = [sb("words%d" % o, [P, T], U32) for o in range(PASSES)]
-        planes = sb("planes", [P, T], U8)
+        words = {}
+        scale_rows = sb("scale_rows", [P, T], U8)
         w1_raw = sb("w1_raw", [P, PASSES, PACK, M], F32)
-        w2_raw = [sb("w2_raw%d" % o, [P, 1, PACK, M], F32) for o in range(PASSES)]
+        w2_first = sb("w2_first", [P, 1, PACK, M], F32)
         fov_cols = sb("fov_cols", [P, 2 * D], F32)
         fov_rows = sb("fov_rows", [P, D, V], F32)
         ident = sb("ident", [P, P], F32)
-        vel_sb = sb("vel_sb", [P, V], F32)
-        want_sb = sb("want_sb", [P, V], F32)
         rad_sb = sb("rad_sb", [P, 1], F32)
         relax_sb = sb("relax_sb", [P, 1], F32)
 
         ones = sb("ones", [P, R], F32)
         ratio = sb("ratio", [P, R], F32)
         warm = sb("warm", [P, 1], F32)
-        nc.gpsimd.memset(planes[:, 0 : T // 2].bitcast(I32), 0)
-        nc.vector.memset(planes[:, T // 2 : T].bitcast(I32), 0)
+        nc.gpsimd.memset(scale_rows[:, 0 : T // 2].bitcast(I32), 0)
+        nc.vector.memset(scale_rows[:, T // 2 : T].bitcast(I32), 0)
         nc.vector.memset(ones[:], 1.0)
         nc.scalar.activation(warm[:], ones[:, 0:1], ACT.Abs_reciprocal_sqrt)
-        nc.vector.tensor_scalar(ratio[:], ones[:], 0.7 / 0.3, None, ALU.mult)
+        nc.vector.tensor_scalar(ratio[:], ones[:], 0.7 / KEPT, None, ALU.mult)
 
-        def load_words(o):
+        def load_words(o, tag=None):
+            words[o] = sb("words%d" % o, [P, T], U32, tag)
             nc.sync.dma_start(words[o][:].bitcast(I32), x_words[o].rearrange("p n t -> p (n t)").bitcast(I32))
 
-        def load_w(raw, rows):
+        def load_w(raw, w_rows):
             nc.sync.dma_start(
-                raw[:].rearrange("p o j n -> p o (j n)"), rows.rearrange("(o p j) n -> p o (j n)", p=P, j=PACK)
+                raw.rearrange("p o j n -> p o (j n)"), w_rows.rearrange("(o p j) n -> p o (j n)", p=P, j=PACK)
             )
 
-        load_words(0)
+        for o in range(PASSES):
+            nc.sync.dma_start(scale_rows[ROWS * o : P : 2 * ROWS, :].bitcast(I32), x_scales[o].bitcast(I32))
         nc.sync.dma_start(offs_sb[:], offs)
-        nc.sync.dma_start(fov_cols[:], fov[0, :].rearrange("(p e) -> p e", p=P))
-        load_w(w1_raw, w1)
-        for q in range(4):
-            nc.sync.dma_start(
-                planes[32 * q : 32 * q + 4 * PASSES, :].bitcast(I32),
-                x_scales[:, 4 * q : 4 * q + 4, :].bitcast(I32),
-            )
-        load_w(w2_raw[0], w2[0:K_PASS, :])
-        load_words(1)
-        nc.sync.dma_start(relax_sb[:], relax)
-        load_w(w2_raw[1], w2[K_PASS:K, :])
-        nc.sync.dma_start(vel_sb[:], vel)
-        nc.sync.dma_start(want_sb[:], want)
-        nc.sync.dma_start(rad_sb[:], rad)
         nc.sync.dma_start(who_sb[:], who)
         nc.sync.dma_start(lead_sb[:], lead)
+        load_w(w1_raw[:], w1)
+        nc.sync.dma_start(fov_cols[:], fov[0, :].rearrange("(p e) -> p e", p=P))
+        nc.sync.dma_start(relax_sb[:], relax)
+        nc.sync.dma_start(rad_sb[:], rad)
+        load_w(w2_first[:], w2[0:K_PASS, :])
+        load_words(0)
+
+        picked_rows = sb("picked_rows", [P, S], U8)
+        planes = sb("planes", [P, S], U8)
+        nc.vector.tensor_copy(picked_rows[:], scale_rows[:].indirect(offs_sb[:]))
+        nc.vector.tensor_copy(planes[:].bitcast(I32), picked_rows[:].bitcast(I32))
+        for o in range(PASSES):
+            for r in range(1, ROWS):
+                nc.sync.dma_start(
+                    planes[ROWS * o + r : P : QUADRANT, :].bitcast(I32),
+                    planes[ROWS * o + 2 * ROWS * r : P : QUADRANT, :].bitcast(I32),
+                )
+        load_words(1, "picked_rows")
 
         def round_w(name, raw):
             rounded = sb(name, [P, raw.shape[1], M, PACK], BF16)
             nc.scalar.copy(
                 rounded[:].rearrange("p o (c e) j -> p o c j e", e=4),
-                raw[:].rearrange("p o j (c e) -> p o c j e", e=4),
+                raw.rearrange("p o j (c e) -> p o c j e", e=4),
             )
             return rounded
 
@@ -106,9 +116,8 @@ def tile_picked_ysocf_lead_p_kernel(
             return [(codes[:, o * M : (o + 1) * M], scales[:, o * M : (o + 1) * M]) for o in range(passes)]
 
         picked = {}
-        picked_planes = [sb("picked_planes%d" % h, [P, HALF], U8) for h in range(HALVES)]
         banks = [[psum.tile([M, BANK], F32, name="bank%d%d" % (i, q)) for q in range(QUARTERS)] for i in range(2)]
-        acc = [[banks[i][q][:, 0:QUARTER] for q in range(QUARTERS)] for i in range(2)]
+        y_acc, z_acc = ([bank[:, 0:QUARTER] for bank in row] for row in banks)
 
         make_identity(nc, ident[:])
         for b in range(2):
@@ -120,100 +129,95 @@ def tile_picked_ysocf_lead_p_kernel(
                 fov_rows[:, 2 * b : 2 * b + 2, :].rearrange("p d (w u) -> p d w u", u=2),
                 spread[:].rearrange("p (u d w) -> p d w u", u=2, d=2),
                 ACT.Copy,
-                scale=0.3 * 1.5,
+                scale=KEPT * 1.5,
             )
 
-        def entries(h):
-            return offs_sb[:, h * HALF // GROUP : (h + 1) * HALF // GROUP]
+        def pick_words(o, h):
+            picked[o, h] = sb("picked%d%d" % (o, h), [P, HALF], U32)
+            entries = offs_sb[:, h * HALF // GROUP : (h + 1) * HALF // GROUP]
+            nc.vector.tensor_copy(picked[o, h][:], words[o][:].indirect(entries))
 
-        def pick_words(o, h, tag=None):
-            picked[o, h] = sb("picked%d%d" % (o, h), [P, HALF], U32, tag)
-            nc.vector.tensor_copy(picked[o, h][:], words[o][:].indirect(entries(h)))
-
-        def pick_planes(h):
-            nc.vector.tensor_copy(picked_planes[h][:], planes[:].indirect(entries(h)))
-
-        def product(i, o, q, weights):
+        def product(acc, o, q, weights):
             h, cols = q // 2, slice(q % 2 * QUARTER, (q % 2 + 1) * QUARTER)
             nc.tensor.matmul_mx(
-                acc[i][q],
+                acc[q],
                 lhsT=weights[o][0].bitcast(FP8X4),
                 lhsT_scale=weights[o][1],
                 rhs=picked[o, h][:, cols].bitcast(FP8X4),
-                rhs_scale=picked_planes[h][4 * o : P, cols],
+                rhs_scale=planes[ROWS * o : P, q * QUARTER : (q + 1) * QUARTER],
                 start=(o == 0),
                 stop=(o == PASSES - 1),
             )
 
-        w1_rounded = round_w("w1_rounded", w1_raw)
-        w2_rounded = [round_w("w2_rounded%d" % o, w2_raw[o]) for o in range(PASSES)]
+        w1_mx = quantize_w("w1", round_w("w1_rounded", w1_raw[:]))
+        w2_mx = quantize_w("w20", round_w("w2_rounded0", w2_first[:]))
         for h in range(HALVES):
             pick_words(0, h)
-        w1_mx = quantize_w("w1", w1_rounded)
-        w2_mx = quantize_w("w20", w2_rounded[0])
-        for h in range(HALVES):
-            pick_planes(h)
             for q in (2 * h, 2 * h + 1):
-                product(0, 0, q, w1_mx)
-                product(1, 0, q, w2_mx)
+                product(y_acc, 0, q, w1_mx)
+                product(z_acc, 0, q, w2_mx)
+
+        late = sb("late", [P, PACK * M + 2 * V], F32, "words0")
+        w2_last = late[:, 0 : PACK * M].rearrange("p (o j n) -> p o j n", o=1, j=PACK)
+        vel_sb = late[:, PACK * M : PACK * M + V]
+        want_sb = late[:, PACK * M + V : PACK * M + 2 * V]
+        load_w(w2_last, w2[K_PASS:K, :])
+        nc.sync.dma_start(vel_sb, vel)
+        nc.sync.dma_start(want_sb, want)
+        w2_rounded = round_w("w2_rounded1", w2_last)
+
         for h in range(HALVES):
             pick_words(1, h)
             for q in (2 * h, 2 * h + 1):
-                product(0, 1, q, w1_mx)
-        w2_mx = w2_mx + quantize_w("w21", w2_rounded[1])
+                product(y_acc, 1, q, w1_mx)
+        w2_mx = w2_mx + quantize_w("w21", w2_rounded)
         for q in range(QUARTERS):
-            product(1, 1, q, w2_mx)
-
-        VQ = QUARTER // D
-        VH = HALF // D
-
-        def pieces(name, count, width):
-            return [sb("%s%d" % (name, n), [P, D, width], F32) for n in range(count)]
-
-        z_sq = pieces("z_sq", QUARTERS, VQ)
-        ssq, inv = (pieces(n, HALVES, VH) for n in ("ssq", "inv"))
-        dist = sb("dist", [P, D, V], F32)
-        pull = sb("pull", [P, D, V], F32)
-        decay = [sb("decay%d" % d, [P, V], F32) for d in range(D)]
-        force = [sb("force%d" % d, [P, V], F32) for d in range(D)]
-        partial = [sb("partial%d" % d, [P, V], F32) for d in range(D)]
+            product(z_acc, 1, q, w2_mx)
 
         c_want = sb("c_want", [P, 1], F32)
         c_vel = sb("c_vel", [P, 1], F32)
         vel_part = sb("vel_part", [P, V], F32)
-        base = sb("base", [P, V], F32, "w2_rounded1")
-        own = sb("own", [P, R], F32)
-        result = sb("result", [P, R], F32)
-        nc.gpsimd.tensor_scalar(c_want[:], relax_sb[:], 0.3, 0.0, ALU.mult, ALU.add)
-        nc.gpsimd.tensor_scalar(c_vel[:], relax_sb[:], -0.3, 0.3, ALU.mult, ALU.add)
-        nc.scalar.activation(vel_part[:], vel_sb[:], ACT.Copy, scale=c_vel[:])
         want_part = sb("want_part", [P, V], F32)
-        nc.scalar.activation(want_part[:], want_sb[:], ACT.Copy, scale=c_want[:])
+        base = sb("base", [P, V], F32, "w2_rounded1")
+        nc.gpsimd.tensor_scalar(c_want[:], relax_sb[:], KEPT, 0.0, ALU.mult, ALU.add)
+        nc.gpsimd.tensor_scalar(c_vel[:], relax_sb[:], -KEPT, KEPT, ALU.mult, ALU.add)
+        nc.scalar.activation(vel_part[:], vel_sb, ACT.Copy, scale=c_vel[:])
+        nc.scalar.activation(want_part[:], want_sb, ACT.Copy, scale=c_want[:])
         nc.gpsimd.tensor_tensor(base[:], want_part[:], vel_part[:], ALU.add)
-
-        y_sq = [sb("y_sq%d" % h, [P, 2, D, VQ], F32, ("vel_sb", "want_sb")[h]) for h in range(HALVES)]
 
         def by_neighbour(bank):
             return bank.rearrange("p (v d) -> p d v", d=D)
 
+        y_sq = sb("y_sq", [P, QUARTERS, D, VQ], F32, "words0")
+        z_sq = [sb("z_sq%d" % q, [P, D, VQ], F32) for q in range(QUARTERS)]
+        ssq = [sb("ssq%d" % h, [P, D, VH], F32) for h in range(HALVES)]
+        inv = [sb("inv%d" % h, [P, D, VH], F32) for h in range(HALVES)]
         for q in range(QUARTERS):
-            nc.scalar.activation(y_sq[q // 2][:, q % 2], by_neighbour(acc[0][q]), ACT.Square)
+            nc.scalar.activation(y_sq[:, q], by_neighbour(y_acc[q]), ACT.Square)
         for q in range(QUARTERS):
-            h, cols = q // 2, slice(q % 2 * VQ, (q % 2 + 1) * VQ)
-            nc.scalar.activation(z_sq[q][:], by_neighbour(acc[1][q]), ACT.Square)
-            nc.vector.scalar_tensor_tensor(ssq[h][:, :, cols], y_sq[h][:, q % 2], 0.1, z_sq[q][:], ALU.add, ALU.add)
-        y_fov_head = sb("y_fov_head", [P, D, V - VQ], F32)
+            walkers = slice(q % 2 * VQ, (q % 2 + 1) * VQ)
+            nc.scalar.activation(z_sq[q][:], by_neighbour(z_acc[q]), ACT.Square)
+            nc.vector.scalar_tensor_tensor(ssq[q // 2][:, :, walkers], y_sq[:, q], 0.1, z_sq[q][:], ALU.add, ALU.add)
+        y_fov_head = sb("y_fov_head", [P, D, V_HEAD], F32)
         y_fov_last = sb("y_fov_last", [P, D, VQ], F32, "z_sq%d" % (QUARTERS - 1))
         for q in range(QUARTERS):
-            dst = y_fov_last[:] if q == QUARTERS - 1 else y_fov_head[:, :, q * VQ : (q + 1) * VQ]
-            nc.vector.tensor_tensor(dst, by_neighbour(acc[0][q]), fov_rows[:, :, q * VQ : (q + 1) * VQ], ALU.mult)
+            y_fov = y_fov_last[:] if q == QUARTERS - 1 else y_fov_head[:, :, q * VQ : (q + 1) * VQ]
+            nc.vector.tensor_tensor(y_fov, by_neighbour(y_acc[q]), fov_rows[:, :, q * VQ : (q + 1) * VQ], ALU.mult)
+
+        dist = sb("dist", [P, D, V], F32)
+        pull = sb("pull", [P, D, V], F32)
         for h in range(HALVES):
             nc.scalar.activation(inv[h][:], ssq[h][:], ACT.Abs_reciprocal_sqrt)
             nc.vector.tensor_tensor(dist[:, :, h * VH : (h + 1) * VH], ssq[h][:], inv[h][:], ALU.mult)
+        warm_exp = sb("warm_exp", [P, 1], F32)
+        nc.scalar.activation(warm_exp[:], inv[HALVES - 1][:, 0, 0:1], ACT.Exp)
         nc.vector.tensor_tensor(pull[:, :, 0:VH], y_fov_head[:, :, 0:VH], inv[0][:], ALU.mult)
-        nc.vector.tensor_tensor(pull[:, :, VH : V - VQ], y_fov_head[:, :, VH : V - VQ], inv[1][:, :, 0:VQ], ALU.mult)
-        nc.vector.tensor_tensor(pull[:, :, V - VQ : V], y_fov_last[:], inv[1][:, :, VQ:VH], ALU.mult)
+        nc.vector.tensor_tensor(pull[:, :, VH:V_HEAD], y_fov_head[:, :, VH:V_HEAD], inv[1][:, :, 0:VQ], ALU.mult)
+        nc.vector.tensor_tensor(pull[:, :, V_HEAD:V], y_fov_last[:], inv[1][:, :, VQ:VH], ALU.mult)
 
+        decay = [sb("decay%d" % d, [P, V], F32) for d in range(D)]
+        force = [sb("force%d" % d, [P, V], F32) for d in range(D)]
+        partial = [sb("partial%d" % d, [P, V], F32) for d in range(D)]
         for d in range(D):
             nc.scalar.activation(decay[d][:], dist[:, d, :], ACT.Exp, bias=rad_sb[:], scale=-1.0)
 
@@ -228,11 +232,14 @@ def tile_picked_ysocf_lead_p_kernel(
             multiply(d)
             add_up(d - 1)
         add_up(D - 1)
-        new_vel = partial[D - 1]
-        walkers = [slice(n * R // 2, (n + 1) * R // 2) for n in range(2)]
-        columns = [slice(n * R // 2 // GROUP, (n + 1) * R // 2 // GROUP) for n in range(2)]
-        for cols, picks in zip(walkers, columns):
-            nc.vector.tensor_tensor(own[:, cols], new_vel[:].indirect(who_sb[:, picks]), ratio[:, cols], ALU.mult)
-        for cols, picks in zip(walkers, columns):
-            nc.vector.tensor_tensor(result[:, cols], new_vel[:].indirect(lead_sb[:, picks]), own[:, cols], ALU.add)
+        kept_nv = partial[D - 1]
+
+        own = sb("own", [P, R], F32)
+        result = sb("result", [P, R], F32)
+        out_cols = [slice(n * R // 2, (n + 1) * R // 2) for n in range(2)]
+        list_cols = [slice(n * R // 2 // GROUP, (n + 1) * R // 2 // GROUP) for n in range(2)]
+        for cols, picks in zip(out_cols, list_cols):
+            nc.vector.tensor_tensor(own[:, cols], kept_nv[:].indirect(who_sb[:, picks]), ratio[:, cols], ALU.mult)
+        for cols, picks in zip(out_cols, list_cols):
+            nc.vector.tensor_tensor(result[:, cols], kept_nv[:].indirect(lead_sb[:, picks]), own[:, cols], ALU.add)
         nc.sync.dma_start(out, result[:])

from contextlib import ExitStack

import concourse.mybir as mybir
from concourse.masks import make_identity

F32 = mybir.dt.float32
BF16 = mybir.dt.bfloat16
I32 = mybir.dt.int32
U32 = mybir.dt.uint32
U16 = mybir.dt.uint16
U8 = mybir.dt.uint8
FP8X4 = mybir.dt.float8_e4m3fn_x4
ALU = mybir.AluOpType
ACT = mybir.ActivationFunctionType

P = 128
K, T, S, D, M, V, R = 1024, 4096, 1024, 4, 128, 256, 128
PACK = 4
K_PASS = P * PACK
PASSES = K // K_PASS
GROUP = 16
HALF = 512
HALVES = S // HALF
QUARTER = 256
QUARTERS = S // QUARTER
BANK = 512
QUADRANT = 32
ROWS = 4
VQ = QUARTER // D
VH = HALF // D
V_HEAD = V - VQ
KEPT = 0.3

FLOPS = 2 * 2 * K * M * S


def tile_picked_ysocf_lead_p_kernel(
    tc, x_words, x_scales, w1, w2, rad, fov, want, vel, relax, offs, lead, who, out
):
    nc = tc.nc
    with ExitStack() as ctx:
        keep = ctx.enter_context(tc.tile_pool(name="keep", bufs=1))
        psum = ctx.enter_context(tc.psum_pool(name="psum", bufs=1))

        def sb(name, shape, dtype, tag=None):
            return keep.tile(shape, dtype, name=name, tag=tag or name, align_bytes=64)

        offs_sb = sb("offs_sb", [P, S // GROUP], U16)
        who_sb = sb("who_sb", [P, R // GROUP], U16)
        lead_sb = sb("lead_sb", [P, R // GROUP], U16)
        words = {}
        scale_rows = sb("scale_rows", [P, T], U8)
        w1_raw = sb("w1_raw", [P, PASSES, PACK, M], F32)
        w2_first = sb("w2_first", [P, 1, PACK, M], F32)
        fov_cols = sb("fov_cols", [P, 2 * D], F32)
        fov_rows = sb("fov_rows", [P, D, V], F32)
        ident = sb("ident", [P, P], F32)
        rad_sb = sb("rad_sb", [P, 1], F32)
        relax_sb = sb("relax_sb", [P, 1], F32)

        ones = sb("ones", [P, R], F32)
        ratio = sb("ratio", [P, R], F32)
        warm = sb("warm", [P, 1], F32)
        nc.gpsimd.memset(scale_rows[:, 0 : T // 2].bitcast(I32), 0)
        nc.vector.memset(scale_rows[:, T // 2 : T].bitcast(I32), 0)
        nc.vector.memset(ones[:], 1.0)
        nc.scalar.activation(warm[:], ones[:, 0:1], ACT.Abs_reciprocal_sqrt)
        nc.vector.tensor_scalar(ratio[:], ones[:], 0.7 / KEPT, None, ALU.mult)

        def load_words(o, tag=None):
            words[o] = sb("words%d" % o, [P, T], U32, tag)
            nc.sync.dma_start(words[o][:].bitcast(I32), x_words[o].rearrange("p n t -> p (n t)").bitcast(I32))

        def load_w(raw, w_rows):
            nc.sync.dma_start(
                raw.rearrange("p o j n -> p o (j n)"), w_rows.rearrange("(o p j) n -> p o (j n)", p=P, j=PACK)
            )

        for o in range(PASSES):
            nc.sync.dma_start(scale_rows[ROWS * o : P : 2 * ROWS, :].bitcast(I32), x_scales[o].bitcast(I32))
        nc.sync.dma_start(offs_sb[:], offs)
        nc.sync.dma_start(who_sb[:], who)
        nc.sync.dma_start(lead_sb[:], lead)
        load_w(w1_raw[:], w1)
        nc.sync.dma_start(fov_cols[:], fov[0, :].rearrange("(p e) -> p e", p=P))
        nc.sync.dma_start(relax_sb[:], relax)
        nc.sync.dma_start(rad_sb[:], rad)
        load_w(w2_first[:], w2[0:K_PASS, :])
        load_words(0)

        picked_rows = sb("picked_rows", [P, S], U8)
        planes = sb("planes", [P, S], U8)
        nc.vector.tensor_copy(picked_rows[:], scale_rows[:].indirect(offs_sb[:]))
        nc.vector.tensor_copy(planes[:].bitcast(I32), picked_rows[:].bitcast(I32))
        for o in range(PASSES):
            for r in range(1, ROWS):
                nc.sync.dma_start(
                    planes[ROWS * o + r : P : QUADRANT, :].bitcast(I32),
                    planes[ROWS * o + 2 * ROWS * r : P : QUADRANT, :].bitcast(I32),
                )
        load_words(1, "picked_rows")

        def round_w(name, raw):
            rounded = sb(name, [P, raw.shape[1], M, PACK], BF16)
            nc.scalar.copy(
                rounded[:].rearrange("p o (c e) j -> p o c j e", e=4),
                raw.rearrange("p o j (c e) -> p o c j e", e=4),
            )
            return rounded

        def quantize_w(name, rounded):
            passes = rounded.shape[1]
            codes = sb(name + "_codes", [P, passes * M], U32)
            scales = sb(name + "_scales", [P, passes * M], U8)
            nc.vector.quantize_mx(codes[:].bitcast(FP8X4), scales[:], rounded[:].rearrange("p o n j -> p (o n j)"))
            return [(codes[:, o * M : (o + 1) * M], scales[:, o * M : (o + 1) * M]) for o in range(passes)]

        picked = {}
        banks = [[psum.tile([M, BANK], F32, name="bank%d%d" % (i, q)) for q in range(QUARTERS)] for i in range(2)]
        y_acc, z_acc = ([bank[:, 0:QUARTER] for bank in row] for row in banks)

        make_identity(nc, ident[:])
        for b in range(2):
            spread = banks[1][QUARTERS - 2 + b]
            for n, (u, d) in enumerate((u, d) for u in range(2) for d in (2 * b, 2 * b + 1)):
                column = fov_cols[:, D * u + d : D * u + d + 1]
                nc.tensor.transpose(spread[:, n * P : (n + 1) * P], column.to_broadcast([P, P]), ident[:])
            nc.scalar.activation(
                fov_rows[:, 2 * b : 2 * b + 2, :].rearrange("p d (w u) -> p d w u", u=2),
                spread[:].rearrange("p (u d w) -> p d w u", u=2, d=2),
                ACT.Copy,
                scale=KEPT * 1.5,
            )

        def pick_words(o, h):
            picked[o, h] = sb("picked%d%d" % (o, h), [P, HALF], U32)
            entries = offs_sb[:, h * HALF // GROUP : (h + 1) * HALF // GROUP]
            nc.vector.tensor_copy(picked[o, h][:], words[o][:].indirect(entries))

        def product(acc, o, q, weights):
            h, cols = q // 2, slice(q % 2 * QUARTER, (q % 2 + 1) * QUARTER)
            nc.tensor.matmul_mx(
                acc[q],
                lhsT=weights[o][0].bitcast(FP8X4),
                lhsT_scale=weights[o][1],
                rhs=picked[o, h][:, cols].bitcast(FP8X4),
                rhs_scale=planes[ROWS * o : P, q * QUARTER : (q + 1) * QUARTER],
                start=(o == 0),
                stop=(o == PASSES - 1),
            )

        w1_mx = quantize_w("w1", round_w("w1_rounded", w1_raw[:]))
        w2_mx = quantize_w("w20", round_w("w2_rounded0", w2_first[:]))
        for h in range(HALVES):
            pick_words(0, h)
            for q in (2 * h, 2 * h + 1):
                product(y_acc, 0, q, w1_mx)
                product(z_acc, 0, q, w2_mx)

        late = sb("late", [P, PACK * M + 2 * V], F32, "words0")
        w2_last = late[:, 0 : PACK * M].rearrange("p (o j n) -> p o j n", o=1, j=PACK)
        vel_sb = late[:, PACK * M : PACK * M + V]
        want_sb = late[:, PACK * M + V : PACK * M + 2 * V]
        load_w(w2_last, w2[K_PASS:K, :])
        nc.sync.dma_start(vel_sb, vel)
        nc.sync.dma_start(want_sb, want)
        w2_rounded = round_w("w2_rounded1", w2_last)

        for h in range(HALVES):
            pick_words(1, h)
            for q in (2 * h, 2 * h + 1):
                product(y_acc, 1, q, w1_mx)
        w2_mx = w2_mx + quantize_w("w21", w2_rounded)
        for q in range(QUARTERS):
            product(z_acc, 1, q, w2_mx)

        c_want = sb("c_want", [P, 1], F32)
        c_vel = sb("c_vel", [P, 1], F32)
        vel_part = sb("vel_part", [P, V], F32)
        want_part = sb("want_part", [P, V], F32)
        base = sb("base", [P, V], F32, "w2_rounded1")
        nc.gpsimd.tensor_scalar(c_want[:], relax_sb[:], KEPT, 0.0, ALU.mult, ALU.add)
        nc.gpsimd.tensor_scalar(c_vel[:], relax_sb[:], -KEPT, KEPT, ALU.mult, ALU.add)
        nc.scalar.activation(vel_part[:], vel_sb, ACT.Copy, scale=c_vel[:])
        nc.scalar.activation(want_part[:], want_sb, ACT.Copy, scale=c_want[:])
        nc.gpsimd.tensor_tensor(base[:], want_part[:], vel_part[:], ALU.add)

        def by_neighbour(bank):
            return bank.rearrange("p (v d) -> p d v", d=D)

        y_sq = sb("y_sq", [P, QUARTERS, D, VQ], F32, "words0")
        z_sq = [sb("z_sq%d" % q, [P, D, VQ], F32) for q in range(QUARTERS)]
        ssq = [sb("ssq%d" % h, [P, D, VH], F32) for h in range(HALVES)]
        inv = [sb("inv%d" % h, [P, D, VH], F32) for h in range(HALVES)]
        for q in range(QUARTERS):
            nc.scalar.activation(y_sq[:, q], by_neighbour(y_acc[q]), ACT.Square)
        for q in range(QUARTERS):
            walkers = slice(q % 2 * VQ, (q % 2 + 1) * VQ)
            nc.scalar.activation(z_sq[q][:], by_neighbour(z_acc[q]), ACT.Square)
            nc.vector.scalar_tensor_tensor(ssq[q // 2][:, :, walkers], y_sq[:, q], 0.1, z_sq[q][:], ALU.add, ALU.add)
        y_fov_head = sb("y_fov_head", [P, D, V_HEAD], F32)
        y_fov_last = sb("y_fov_last", [P, D, VQ], F32, "z_sq%d" % (QUARTERS - 1))
        for q in range(QUARTERS):
            y_fov = y_fov_last[:] if q == QUARTERS - 1 else y_fov_head[:, :, q * VQ : (q + 1) * VQ]
            nc.vector.tensor_tensor(y_fov, by_neighbour(y_acc[q]), fov_rows[:, :, q * VQ : (q + 1) * VQ], ALU.mult)

        dist = sb("dist", [P, D, V], F32)
        pull = sb("pull", [P, D, V], F32)
        for h in range(HALVES):
            nc.scalar.activation(inv[h][:], ssq[h][:], ACT.Abs_reciprocal_sqrt)
            nc.vector.tensor_tensor(dist[:, :, h * VH : (h + 1) * VH], ssq[h][:], inv[h][:], ALU.mult)
        warm_exp = sb("warm_exp", [P, 1], F32)
        nc.scalar.activation(warm_exp[:], inv[HALVES - 1][:, 0, 0:1], ACT.Exp)
        nc.vector.tensor_tensor(pull[:, :, 0:VH], y_fov_head[:, :, 0:VH], inv[0][:], ALU.mult)
        nc.vector.tensor_tensor(pull[:, :, VH:V_HEAD], y_fov_head[:, :, VH:V_HEAD], inv[1][:, :, 0:VQ], ALU.mult)
        nc.vector.tensor_tensor(pull[:, :, V_HEAD:V], y_fov_last[:], inv[1][:, :, VQ:VH], ALU.mult)

        decay = [sb("decay%d" % d, [P, V], F32) for d in range(D)]
        force = [sb("force%d" % d, [P, V], F32) for d in range(D)]
        partial = [sb("partial%d" % d, [P, V], F32) for d in range(D)]
        for d in range(D):
            nc.scalar.activation(decay[d][:], dist[:, d, :], ACT.Exp, bias=rad_sb[:], scale=-1.0)

        def multiply(d):
            nc.vector.tensor_tensor(force[d][:], pull[:, d, :], decay[d][:], ALU.mult)

        def add_up(d):
            nc.vector.tensor_tensor(partial[d][:], force[d][:], partial[d - 1][:] if d else base[:], ALU.add)

        multiply(0)
        for d in range(1, D):
            multiply(d)
            add_up(d - 1)
        add_up(D - 1)
        kept_nv = partial[D - 1]

        own = sb("own", [P, R], F32)
        result = sb("result", [P, R], F32)
        out_cols = [slice(n * R // 2, (n + 1) * R // 2) for n in range(2)]
        list_cols = [slice(n * R // 2 // GROUP, (n + 1) * R // 2 // GROUP) for n in range(2)]
        for cols, picks in zip(out_cols, list_cols):
            nc.vector.tensor_tensor(own[:, cols], kept_nv[:].indirect(who_sb[:, picks]), ratio[:, cols], ALU.mult)
        for cols, picks in zip(out_cols, list_cols):
            nc.vector.tensor_tensor(result[:, cols], kept_nv[:].indirect(lead_sb[:, picks]), own[:, cols], ALU.add)
        nc.sync.dma_start(out, result[:])
